import numpy as np
CORES = [3,0,2,1,6,7,4,5]
N = 8
ROUNDS = 4
def setup_inputs(rng):
    return {"x": rng.standard_normal((N, ROUNDS, 128, 128), dtype=np.float32)}
def reference(x):
    b = 128 // N
    bl = x.reshape(N, ROUNDS, 128, N, b)
    return {"y": np.ascontiguousarray(bl.transpose(3, 1, 2, 0, 4)).reshape(N, ROUNDS, 128, 128)}

@@ -1,0 +1,43 @@
+SCRATCH = {
+    "send": ("sbuf", [128, 128], "float32"),
+    "land": ("sbuf", [128, 128], "float32"),
+}
+SEMAPHORES = ["loaded", "read", "arrived", "stored", "credit"]
+
+B = 16
+
+
+def rank_program(g, core, T, topo):
+    rank = T.rank_of(core)
+    if rank is None:
+        return
+    n = len(T.cores)
+    rounds = T.x.shape[0]
+    peers = [j for j in range(n) if j != rank]
+    loaded = stored = read = 0
+    for k in range(rounds):
+        if k:
+            g.wait_ge(T.sem.read, read)
+        g.dma_start(T.send[:], T.x[k]).then_inc(T.sem.loaded, 16)
+        g.dma_start(T.land[:, rank * B:(rank + 1) * B], T.x[k][:, rank * B:(rank + 1) * B]).then_inc(T.sem.loaded, 16)
+        loaded += 32
+        g.wait_ge(T.sem.loaded, loaded)
+        if k:
+            g.wait_ge(T.sem.credit, k * len(peers))
+        for j in peers:
+            dst = T.cores[j]
+            rid, pid, se = topo.addr(dst)
+            g.remote_dma(T.land[:, rank * B:(rank + 1) * B], T.send[:, j * B:(j + 1) * B], T.sem.arrived, T.sem.read,
+                         pid, rid, topo.mask(core, dst))
+            read += 16
+        g.wait_ge(T.sem.arrived, 16 * len(peers) * (k + 1))
+        g.dma_start(T.y[k], T.land[:]).then_inc(T.sem.stored, 16)
+        stored += 16
+        g.wait_ge(T.sem.stored, stored)
+        if k + 1 < rounds:
+            for j in peers:
+                dst = T.cores[j]
+                rid, pid, se = topo.addr(dst)
+                g.remote_sem_update(T.sem.credit, T.sem.read, pid, rid, 1)
+                read += 1
+    g.wait_ge(T.sem.read, read)

@@ -1,10 +1,12 @@
-SCRATCH = {
-    "send": ("sbuf", [128, 128], "float32"),
-    "land": ("sbuf", [128, 128], "float32"),
-}
-SEMAPHORES = ["loaded", "read", "arrived", "stored", "credit"]
+from concourse.bass import DstId, RemoteDMATransfer
 
-B = 16
+SCRATCH = {
+    "a": ("sbuf", [128, 128], "float32"),
+    "b": ("sbuf", [128, 128], "float32"),
+}
+SEMAPHORES = ["loaded", "stored", "left", "even", "odd"]
+
+ENGINES = 2
 
 
 def rank_program(g, core, T, topo):
@@ -13,31 +15,30 @@ def rank_program(g, core, T, topo):
         return
     n = len(T.cores)
     rounds = T.x.shape[0]
-    peers = [j for j in range(n) if j != rank]
-    loaded = stored = read = 0
+    w = T.x.shape[2] // n
+    bufs = [T.a, T.b]
+    arrived = [T.sem.even, T.sem.odd]
+    peers = [(rank + s) % n for s in range(1, n)]
+    per_round = ENGINES * len(peers)
+    mine = slice(rank * w, (rank + 1) * w)
+
     for k in range(rounds):
-        if k:
-            g.wait_ge(T.sem.read, read)
-        g.dma_start(T.send[:], T.x[k]).then_inc(T.sem.loaded, 16)
-        g.dma_start(T.land[:, rank * B:(rank + 1) * B], T.x[k][:, rank * B:(rank + 1) * B]).then_inc(T.sem.loaded, 16)
-        loaded += 32
-        g.wait_ge(T.sem.loaded, loaded)
-        if k:
-            g.wait_ge(T.sem.credit, k * len(peers))
-        for j in peers:
-            dst = T.cores[j]
-            rid, pid, se = topo.addr(dst)
-            g.remote_dma(T.land[:, rank * B:(rank + 1) * B], T.send[:, j * B:(j + 1) * B], T.sem.arrived, T.sem.read,
-                         pid, rid, topo.mask(core, dst))
-            read += 16
-        g.wait_ge(T.sem.arrived, 16 * len(peers) * (k + 1))
-        g.dma_start(T.y[k], T.land[:]).then_inc(T.sem.stored, 16)
-        stored += 16
-        g.wait_ge(T.sem.stored, stored)
-        if k + 1 < rounds:
-            for j in peers:
-                dst = T.cores[j]
-                rid, pid, se = topo.addr(dst)
-                g.remote_sem_update(T.sem.credit, T.sem.read, pid, rid, 1)
-                read += 1
-    g.wait_ge(T.sem.read, read)
+        send, land = bufs[k % 2], bufs[(k + 1) % 2]
+        g.dma_start(send[:], T.x[k]).then_inc(T.sem.loaded, 16)
+        g.dma_start(land[:, mine], T.x[k][:, mine]).then_inc(T.sem.loaded, 16)
+        g.wait_ge(T.sem.loaded, 32 * (k + 1))
+        transfers = []
+        for i, j in enumerate(peers):
+            rid, pid, sengine = topo.addr(T.cores[j])
+            transfers.append(RemoteDMATransfer(
+                dst_ids=[DstId(rid=rid, pnc=pid)],
+                dma_engine_mask=((1 << ENGINES) - 1) << (ENGINES * i),
+                remote_sem=arrived[k % 2],
+                src=send[:, j * w:(j + 1) * w],
+                dst=land[:, mine],
+            ))
+        g.remote_dma_fused(transfers, local_sem=T.sem.left)
+        g.wait_ge(arrived[k % 2], per_round * (k // 2 + 1))
+        g.wait_ge(T.sem.left, per_round * (k + 1))
+        g.dma_start(T.y[k], land[:]).then_inc(T.sem.stored, 16)
+        g.wait_ge(T.sem.stored, 16 * (k + 1))

from concourse.bass import DstId, RemoteDMATransfer

SCRATCH = {
    "a": ("sbuf", [128, 128], "float32"),
    "b": ("sbuf", [128, 128], "float32"),
}
SEMAPHORES = ["loaded", "stored", "left", "even", "odd"]

ENGINES = 2


def rank_program(g, core, T, topo):
    rank = T.rank_of(core)
    if rank is None:
        return
    n = len(T.cores)
    rounds = T.x.shape[0]
    w = T.x.shape[2] // n
    bufs = [T.a, T.b]
    arrived = [T.sem.even, T.sem.odd]
    peers = [(rank + s) % n for s in range(1, n)]
    per_round = ENGINES * len(peers)
    mine = slice(rank * w, (rank + 1) * w)

    for k in range(rounds):
        send, land = bufs[k % 2], bufs[(k + 1) % 2]
        g.dma_start(send[:], T.x[k]).then_inc(T.sem.loaded, 16)
        g.dma_start(land[:, mine], T.x[k][:, mine]).then_inc(T.sem.loaded, 16)
        g.wait_ge(T.sem.loaded, 32 * (k + 1))
        transfers = []
        for i, j in enumerate(peers):
            rid, pid, sengine = topo.addr(T.cores[j])
            transfers.append(RemoteDMATransfer(
                dst_ids=[DstId(rid=rid, pnc=pid)],
                dma_engine_mask=((1 << ENGINES) - 1) << (ENGINES * i),
                remote_sem=arrived[k % 2],
                src=send[:, j * w:(j + 1) * w],
                dst=land[:, mine],
            ))
        g.remote_dma_fused(transfers, local_sem=T.sem.left)
        g.wait_ge(arrived[k % 2], per_round * (k // 2 + 1))
        g.wait_ge(T.sem.left, per_round * (k + 1))
        g.dma_start(T.y[k], land[:]).then_inc(T.sem.stored, 16)
        g.wait_ge(T.sem.stored, 16 * (k + 1))
